import numpy as np
import ml_dtypes


def mxq(x, axis, fmt="e4m3"):
    dtype, down = {"e4m3": (ml_dtypes.float8_e4m3fn, 7), "e5m2": (ml_dtypes.float8_e5m2, 14)}[fmt]
    v = np.moveaxis(np.asarray(x, np.float32).astype(ml_dtypes.bfloat16).astype(np.float64), axis, -1)
    blocks = v.reshape(v.shape[:-1] + (-1, 32))
    amax = np.abs(blocks).max(-1, keepdims=True)
    byte = np.maximum(np.where(amax > 0, np.frexp(amax)[1] - 1 + 127, 0) - down, 1)
    scale = np.exp2(byte - 127.0)
    codes = (blocks / scale).astype(np.float32).astype(dtype).astype(np.float64)
    return np.moveaxis((codes * scale).reshape(v.shape), -1, axis)


WIDE = False


def mx_kscale(k):
    if not WIDE:
        return np.ones(k)
    levels = np.array([10, -10, 5, -5, 0])
    if k % 512:
        return np.exp2(np.random.permutation(np.resize(levels, k // 32))).repeat(32)
    a = np.empty((k // 512, 16))
    for p in range(k // 512):
        a[p, :8] = np.random.permutation(np.resize(levels, 8))
        for g in range(8):
            far = levels[np.abs(levels - a[p, g]) >= 10]
            a[p, g + 8] = far[np.random.randint(len(far))]
    return np.exp2(a.ravel()).repeat(32)


def f64(x):
    return np.asarray(x).astype(np.float64)


def striped(idx):
    return np.tile(idx.reshape(-1, 16).T, (8, 1)).astype(np.uint16)


def unstriped(offs):
    return offs[:16].T.reshape(-1).astype(np.int64)


def pack_weight(w):
    k, n = w.shape
    w = f64(np.asarray(w, np.float32).astype(ml_dtypes.bfloat16)).reshape(k // 32, 32, n)
    amax = np.abs(w).max(1)
    byte = np.clip(np.where(amax > 0, np.frexp(amax)[1] - 1 + 127 - 7, 1), 1, 254)
    scaled = (w * np.exp2(127.0 - byte)[:, None, :]).reshape(k, n).astype(np.float32)
    words = np.ascontiguousarray(scaled.reshape(k // 512, 128, 4, n).transpose(0, 1, 3, 2)).astype(ml_dtypes.float8_e4m3fn).view(np.uint8)
    return words, np.ascontiguousarray(byte.astype(np.uint8).reshape(k // 512, 16, n))


def unpack_weight(words, scales):
    g, p, n, _ = words.shape
    vals = np.ascontiguousarray(words).view(ml_dtypes.float8_e4m3fn).astype(np.float64) * np.repeat(np.exp2(scales.astype(np.float64) - 127.0), 8, axis=1)[..., None]
    return vals.transpose(0, 1, 3, 2).reshape(g * 512, n)


def sigmoid(v):
    return 1.0 / (1.0 + np.exp(-np.maximum(v, -700.0)))


K, T, S, N = 512, 1024, 512, 128


def setup_inputs():
    n = np.random.standard_normal
    s = mx_kscale(K)[:, None]
    packed_xT = pack_weight(n((K, T)) * s)
    return {
        "x_words": packed_xT[0],
        "x_scales": packed_xT[1],
        "w1": (n((K, N)) / np.sqrt(K) / s).astype(np.float32),
        "mob": (np.random.uniform(0.05, 0.25, (N, 1))).astype(np.float32),
        "offs": striped(np.random.permutation(T)[:S]),
        "pos1": striped(np.random.permutation(S)[:S]),
        "pos2": striped(np.random.permutation(S)[:S]),
        "pos3": striped(np.random.permutation(S)[:S]),
    }


def reference(x_words, x_scales, w1, mob, offs, pos1, pos2, pos3):
    xq = unpack_weight(x_words, x_scales)[:, unstriped(offs)]
    y = mxq(f64(w1), 0, "e4m3").T @ xq
    con = 0.9 * sigmoid(y)
    mu = 0.4 * (np.log((con + 0.05) / (-1.0 * con + 0.95))) - con - (0.2 * (con[:, unstriped(pos1)] + con[:, unstriped(pos2)] + con[:, unstriped(pos3)] - (3.0 * con)))
    return con + f64(mob) * (mu[:, unstriped(pos1)] + mu[:, unstriped(pos2)] + mu[:, unstriped(pos3)] - (3.0 * mu))

@@ -1,0 +1,119 @@
+from contextlib import ExitStack
+import math
+
+import concourse.mybir as mybir
+
+K, T, S, N = 512, 1024, 512, 128
+FLOPS = 2 * K * S * N
+
+F32 = mybir.dt.float32
+BF16 = mybir.dt.bfloat16
+I32 = mybir.dt.int32
+U32 = mybir.dt.uint32
+U16 = mybir.dt.uint16
+U8 = mybir.dt.uint8
+FP8X4 = mybir.dt.float8_e4m3fn_x4
+ACT = mybir.ActivationFunctionType
+ALU = mybir.AluOpType
+
+P = 128
+PACK = 4
+GROUP = 16
+PRODUCT_SLICES = ((0, 256), (256, 384), (384, 512))
+HALVES = ((0, 256), (256, 512))
+
+
+def tile_picked_ycahnh_log_p_kernel(tc, x_words, x_scales, w1, mob, offs, pos1, pos2, pos3, out):
+    nc = tc.nc
+    with ExitStack() as ctx:
+        lists = ctx.enter_context(tc.tile_pool(name="lists", bufs=1))
+        keep = ctx.enter_context(tc.tile_pool(name="keep", bufs=1))
+        psum = ctx.enter_context(tc.psum_pool(name="psum", bufs=1))
+
+        def entries(tile, lo, hi):
+            return tile[:, lo // GROUP : hi // GROUP]
+
+        picked = lists.tile([P, S // GROUP], U16, name="picked")
+        neighbours = [lists.tile([P, S // GROUP], U16, name="neighbours%d" % i) for i in range(3)]
+        nc.sync.dma_start(picked[:], offs)
+        w_raw = keep.tile([P, PACK, N], F32, name="w_raw")
+        nc.scalar.dma_start(out=w_raw[:], in_=w1.rearrange("(p j) n -> p j n", j=PACK))
+        scale_table = keep.tile([P, T], U8, name="scale_table", align_bytes=64)
+        nc.vector.memset(scale_table[:, : T // 2].bitcast(I32), 0)
+        nc.gpsimd.memset(scale_table[:, T // 2 :].bitcast(I32), 0)
+        scale_rows = x_scales[0].bitcast(I32)
+        for q in range(4):
+            (nc.sync if q < 2 else nc.scalar).dma_start(out=scale_table[32 * q : 32 * q + 4, :].bitcast(I32), in_=scale_rows[4 * q : 4 * q + 4, :])
+        word_table = keep.tile([P, T], I32, name="word_table", align_bytes=64)
+        nc.sync.dma_start(out=word_table[:], in_=x_words[0].rearrange("p n t -> p (n t)").bitcast(I32))
+        nc.sync.dma_start(neighbours[0][:], pos1)
+        nc.sync.dma_start(neighbours[1][:], pos2)
+        nc.sync.dma_start(neighbours[2][:], pos3)
+        mobility = keep.tile([P, 1], F32, name="mobility")
+        nc.sync.dma_start(out=mobility[:], in_=mob)
+
+        warm_in = keep.tile([P, 1], F32, name="warm_in")
+        warm_out = keep.tile([P, 1], F32, name="warm_out")
+        nc.vector.memset(warm_in[:], 0.0)
+        nc.scalar.activation(warm_out[:], warm_in[:], ACT.Sigmoid)
+
+        x_bytes = keep.tile([P, S], U8, name="x_bytes", align_bytes=64)
+        nc.vector.tensor_copy(x_bytes[:], scale_table[:].indirect(picked[:]))
+
+        w_grouped = keep.tile([P, N, PACK], BF16, name="w_grouped", align_bytes=64)
+        nc.scalar.copy(out=w_grouped[:], in_=w_raw[:].rearrange("p j n -> p n j"))
+        w_codes = keep.tile([P, N], U32, name="w_codes", align_bytes=64)
+        w_bytes = keep.tile([P, N], U8, name="w_bytes", align_bytes=64)
+        nc.vector.quantize_mx(out=w_codes[:].bitcast(FP8X4), scales=w_bytes[:], in_=w_grouped[:].rearrange("p n j -> p (n j)"))
+
+        lap_factor = keep.tile([P, 1], F32, name="lap_factor")
+        log_factor = keep.tile([P, 1], F32, name="log_factor")
+        nc.gpsimd.tensor_scalar(lap_factor[:], mobility[:], -0.18, 0.0, ALU.mult, ALU.add)
+        nc.gpsimd.tensor_scalar(log_factor[:], mobility[:], 0.4, 0.0, ALU.mult, ALU.add)
+
+        x_codes = keep.tile([P, S], U32, name="x_codes", align_bytes=64)
+        sig = keep.tile([P, S], F32, name="sig")
+        shifted = keep.tile([P, S], F32, name="shifted")
+        twice = keep.tile([P, S], F32, name="twice")
+        banks = []
+        for i, (lo, hi) in enumerate(PRODUCT_SLICES):
+            nc.vector.tensor_copy(x_codes[:, lo:hi], word_table[:].bitcast(U32).indirect(entries(picked, lo, hi)))
+            y = psum.tile([P, hi - lo], F32, name="y%d" % i)
+            nc.tensor.matmul_mx(out=y[:], lhsT=w_codes[:].bitcast(FP8X4), lhsT_scale=w_bytes[:], rhs=x_codes[:, lo:hi].bitcast(FP8X4), rhs_scale=x_bytes[:, lo:hi], start=True, stop=True)
+            nc.scalar.activation(sig[:, lo:hi], y[:], ACT.Sigmoid)
+            banks.append(y)
+            if i == 0:
+                nc.scalar.activation(shifted[:, lo:hi], y[:], ACT.Sigmoid, bias=-math.log(19.0))
+        for y, (lo, hi) in zip(banks[1:], PRODUCT_SLICES[1:]):
+            nc.scalar.activation(shifted[:, lo:hi], y[:], ACT.Sigmoid, bias=-math.log(19.0))
+        for lo, hi in HALVES:
+            nc.vector.tensor_scalar(twice[:, lo:hi], sig[:, lo:hi], 2.0, None, ALU.mult)
+
+        log_ratio = keep.tile([P, S], F32, name="log_ratio")
+        log_term = keep.tile([P, S], F32, name="log_term")
+        con = keep.tile([P, S], F32, name="con")
+        for lo, hi in HALVES:
+            nc.scalar.activation(log_ratio[:, lo:hi], shifted[:, lo:hi], ACT.Ln, bias=1.0 / 19.0, scale=360.0 / 19.0)
+            nc.scalar.activation(log_term[:, lo:hi], log_ratio[:, lo:hi], ACT.Copy, scale=log_factor[:])
+        for lo, hi in HALVES:
+            nc.scalar.activation(con[:, lo:hi], sig[:, lo:hi], ACT.Copy, scale=0.9)
+
+        def add_neighbours(window, start, name):
+            total = start
+            for i, places in enumerate(neighbours):
+                following = keep.tile([P, S], F32, name="%s%d" % (name, i))
+                for lo, hi in HALVES:
+                    nc.vector.tensor_tensor(following[:, lo:hi], window[:].indirect(entries(places, lo, hi)), total[:, lo:hi], ALU.add)
+                total = following
+            return total
+
+        sig_sum = add_neighbours(sig, twice, "sig_sum")
+        flux = keep.tile([P, S], F32, name="flux")
+        base = keep.tile([P, S], F32, name="base")
+        for lo, hi in HALVES:
+            nc.vector.scalar_tensor_tensor(flux[:, lo:hi], sig_sum[:, lo:hi], lap_factor[:], log_term[:, lo:hi], ALU.mult, ALU.add)
+        for lo, hi in HALVES:
+            nc.vector.scalar_tensor_tensor(base[:, lo:hi], flux[:, lo:hi], -3.0, con[:, lo:hi], ALU.mult, ALU.add)
+        result = add_neighbours(flux, base, "result")
+        for lo, hi in HALVES:
+            nc.sync.dma_start(out=out[:, lo:hi], in_=result[:, lo:hi])

@@ -19,8 +19,9 @@ ALU = mybir.AluOpType
 P = 128
 PACK = 4
 GROUP = 16
-PRODUCT_SLICES = ((0, 256), (256, 384), (384, 512))
+PRODUCT_SLICES = ((0, 128), (128, 384), (384, 512))
 HALVES = ((0, 256), (256, 512))
+STORE_SLICES = ((0, 256), (256, 416), (416, 512))
 
 
 def tile_picked_ycahnh_log_p_kernel(tc, x_words, x_scales, w1, mob, offs, pos1, pos2, pos3, out):
@@ -33,60 +34,66 @@ def tile_picked_ycahnh_log_p_kernel(tc, x_words, x_scales, w1, mob, offs, pos1, 
         def entries(tile, lo, hi):
             return tile[:, lo // GROUP : hi // GROUP]
 
-        picked = lists.tile([P, S // GROUP], U16, name="picked")
-        neighbours = [lists.tile([P, S // GROUP], U16, name="neighbours%d" % i) for i in range(3)]
-        nc.sync.dma_start(picked[:], offs)
-        w_raw = keep.tile([P, PACK, N], F32, name="w_raw")
-        nc.scalar.dma_start(out=w_raw[:], in_=w1.rearrange("(p j) n -> p j n", j=PACK))
-        scale_table = keep.tile([P, T], U8, name="scale_table", align_bytes=64)
-        nc.vector.memset(scale_table[:, : T // 2].bitcast(I32), 0)
-        nc.gpsimd.memset(scale_table[:, T // 2 :].bitcast(I32), 0)
-        scale_rows = x_scales[0].bitcast(I32)
-        for q in range(4):
-            (nc.sync if q < 2 else nc.scalar).dma_start(out=scale_table[32 * q : 32 * q + 4, :].bitcast(I32), in_=scale_rows[4 * q : 4 * q + 4, :])
         word_table = keep.tile([P, T], I32, name="word_table", align_bytes=64)
         nc.sync.dma_start(out=word_table[:], in_=x_words[0].rearrange("p n t -> p (n t)").bitcast(I32))
-        nc.sync.dma_start(neighbours[0][:], pos1)
-        nc.sync.dma_start(neighbours[1][:], pos2)
-        nc.sync.dma_start(neighbours[2][:], pos3)
+        picked = lists.tile([P, S // GROUP], U16, name="picked")
+        nc.sync.dma_start(picked[:], offs)
+        w_raw = keep.tile([P, PACK, N], F32, name="w_raw")
+        nc.sync.dma_start(out=w_raw[:], in_=w1.rearrange("(p j) n -> p j n", j=PACK))
+        scale_table = keep.tile([P, T], U8, name="scale_table", align_bytes=64)
+        nc.vector.memset(scale_table[:].bitcast(I32), 0)
+        scale_rows = x_scales[0].bitcast(I32)
+        for q in range(4):
+            nc.sync.dma_start(out=scale_table[32 * q : 32 * q + 4, :].bitcast(I32), in_=scale_rows[4 * q : 4 * q + 4, :])
+        neighbours = []
+        for i, pos in enumerate((pos1, pos2, pos3)):
+            tile = lists.tile([P, S // GROUP], U16, name="neighbours%d" % i)
+            nc.sync.dma_start(tile[:], pos)
+            neighbours.append(tile)
         mobility = keep.tile([P, 1], F32, name="mobility")
         nc.sync.dma_start(out=mobility[:], in_=mob)
 
         warm_in = keep.tile([P, 1], F32, name="warm_in")
         warm_out = keep.tile([P, 1], F32, name="warm_out")
-        nc.vector.memset(warm_in[:], 0.0)
+        nc.gpsimd.memset(warm_in[:], 0.0)
         nc.scalar.activation(warm_out[:], warm_in[:], ACT.Sigmoid)
 
-        x_bytes = keep.tile([P, S], U8, name="x_bytes", align_bytes=64)
-        nc.vector.tensor_copy(x_bytes[:], scale_table[:].indirect(picked[:]))
+        x_codes = keep.tile([P, S], U32, name="x_codes", align_bytes=64)
+        nc.vector.tensor_copy(x_codes[:], word_table[:].bitcast(U32).indirect(picked[:]))
 
         w_grouped = keep.tile([P, N, PACK], BF16, name="w_grouped", align_bytes=64)
         nc.scalar.copy(out=w_grouped[:], in_=w_raw[:].rearrange("p j n -> p n j"))
         w_codes = keep.tile([P, N], U32, name="w_codes", align_bytes=64)
         w_bytes = keep.tile([P, N], U8, name="w_bytes", align_bytes=64)
         nc.vector.quantize_mx(out=w_codes[:].bitcast(FP8X4), scales=w_bytes[:], in_=w_grouped[:].rearrange("p n j -> p (n j)"))
+        picked_bytes = keep.tile([P, S], U8, name="picked_bytes", align_bytes=64)
 
         lap_factor = keep.tile([P, 1], F32, name="lap_factor")
         log_factor = keep.tile([P, 1], F32, name="log_factor")
         nc.gpsimd.tensor_scalar(lap_factor[:], mobility[:], -0.18, 0.0, ALU.mult, ALU.add)
         nc.gpsimd.tensor_scalar(log_factor[:], mobility[:], 0.4, 0.0, ALU.mult, ALU.add)
 
-        x_codes = keep.tile([P, S], U32, name="x_codes", align_bytes=64)
         sig = keep.tile([P, S], F32, name="sig")
         shifted = keep.tile([P, S], F32, name="shifted")
         twice = keep.tile([P, S], F32, name="twice")
         banks = []
+
+        def shifted_sigmoid(i):
+            lo, hi = PRODUCT_SLICES[i]
+            nc.scalar.activation(shifted[:, lo:hi], banks[i][:], ACT.Sigmoid, bias=-math.log(19.0))
+
         for i, (lo, hi) in enumerate(PRODUCT_SLICES):
-            nc.vector.tensor_copy(x_codes[:, lo:hi], word_table[:].bitcast(U32).indirect(entries(picked, lo, hi)))
+            x_bytes = picked_bytes[:, lo:hi]
+            nc.vector.tensor_copy(x_bytes, scale_table[:].indirect(entries(picked, lo, hi)))
             y = psum.tile([P, hi - lo], F32, name="y%d" % i)
-            nc.tensor.matmul_mx(out=y[:], lhsT=w_codes[:].bitcast(FP8X4), lhsT_scale=w_bytes[:], rhs=x_codes[:, lo:hi].bitcast(FP8X4), rhs_scale=x_bytes[:, lo:hi], start=True, stop=True)
+            nc.tensor.matmul_mx(out=y[:], lhsT=w_codes[:].bitcast(FP8X4), lhsT_scale=w_bytes[:], rhs=x_codes[:, lo:hi].bitcast(FP8X4), rhs_scale=x_bytes, start=True, stop=True)
             nc.scalar.activation(sig[:, lo:hi], y[:], ACT.Sigmoid)
             banks.append(y)
-            if i == 0:
-                nc.scalar.activation(shifted[:, lo:hi], y[:], ACT.Sigmoid, bias=-math.log(19.0))
-        for y, (lo, hi) in zip(banks[1:], PRODUCT_SLICES[1:]):
-            nc.scalar.activation(shifted[:, lo:hi], y[:], ACT.Sigmoid, bias=-math.log(19.0))
-        for lo, hi in HALVES:
+            if i < 1:
+                shifted_sigmoid(i)
+        for i in (1, 2):
+            shifted_sigmoid(i)
+        for lo, hi in PRODUCT_SLICES:
             nc.vector.tensor_scalar(twice[:, lo:hi], sig[:, lo:hi], 2.0, None, ALU.mult)
 
         log_ratio = keep.tile([P, S], F32, name="log_ratio")
@@ -98,22 +105,22 @@ def tile_picked_ycahnh_log_p_kernel(tc, x_words, x_scales, w1, mob, offs, pos1, 
         for lo, hi in HALVES:
             nc.scalar.activation(con[:, lo:hi], sig[:, lo:hi], ACT.Copy, scale=0.9)
 
-        def add_neighbours(window, start, name):
+        def add_neighbours(window, start, name, last_slices):
             total = start
             for i, places in enumerate(neighbours):
                 following = keep.tile([P, S], F32, name="%s%d" % (name, i))
-                for lo, hi in HALVES:
+                for lo, hi in last_slices if i == 2 else HALVES:
                     nc.vector.tensor_tensor(following[:, lo:hi], window[:].indirect(entries(places, lo, hi)), total[:, lo:hi], ALU.add)
                 total = following
             return total
 
-        sig_sum = add_neighbours(sig, twice, "sig_sum")
+        sig_sum = add_neighbours(sig, twice, "sig_sum", HALVES)
         flux = keep.tile([P, S], F32, name="flux")
         base = keep.tile([P, S], F32, name="base")
         for lo, hi in HALVES:
             nc.vector.scalar_tensor_tensor(flux[:, lo:hi], sig_sum[:, lo:hi], lap_factor[:], log_term[:, lo:hi], ALU.mult, ALU.add)
         for lo, hi in HALVES:
             nc.vector.scalar_tensor_tensor(base[:, lo:hi], flux[:, lo:hi], -3.0, con[:, lo:hi], ALU.mult, ALU.add)
-        result = add_neighbours(flux, base, "result")
-        for lo, hi in HALVES:
+        result = add_neighbours(flux, base, "result", STORE_SLICES)
+        for lo, hi in STORE_SLICES:
             nc.sync.dma_start(out=out[:, lo:hi], in_=result[:, lo:hi])

@@ -19,7 +19,7 @@ ALU = mybir.AluOpType
 P = 128
 PACK = 4
 GROUP = 16
-PRODUCT_SLICES = ((0, 128), (128, 384), (384, 512))
+PRODUCT_SLICES = ((0, 128), (128, 256), (256, 384), (384, 512))
 HALVES = ((0, 256), (256, 512))
 STORE_SLICES = ((0, 256), (256, 416), (416, 512))
 
@@ -38,13 +38,13 @@ def tile_picked_ycahnh_log_p_kernel(tc, x_words, x_scales, w1, mob, offs, pos1, 
         nc.sync.dma_start(out=word_table[:], in_=x_words[0].rearrange("p n t -> p (n t)").bitcast(I32))
         picked = lists.tile([P, S // GROUP], U16, name="picked")
         nc.sync.dma_start(picked[:], offs)
-        w_raw = keep.tile([P, PACK, N], F32, name="w_raw")
-        nc.sync.dma_start(out=w_raw[:], in_=w1.rearrange("(p j) n -> p j n", j=PACK))
         scale_table = keep.tile([P, T], U8, name="scale_table", align_bytes=64)
         nc.vector.memset(scale_table[:].bitcast(I32), 0)
         scale_rows = x_scales[0].bitcast(I32)
         for q in range(4):
             nc.sync.dma_start(out=scale_table[32 * q : 32 * q + 4, :].bitcast(I32), in_=scale_rows[4 * q : 4 * q + 4, :])
+        w_raw = keep.tile([P, PACK, N], F32, name="w_raw", tag="shared", align_bytes=64)
+        nc.sync.dma_start(out=w_raw[:], in_=w1.rearrange("(p j) n -> p j n", j=PACK))
         neighbours = []
         for i, pos in enumerate((pos1, pos2, pos3)):
             tile = lists.tile([P, S // GROUP], U16, name="neighbours%d" % i)
@@ -65,8 +65,10 @@ def tile_picked_ycahnh_log_p_kernel(tc, x_words, x_scales, w1, mob, offs, pos1, 
         nc.scalar.copy(out=w_grouped[:], in_=w_raw[:].rearrange("p j n -> p n j"))
         w_codes = keep.tile([P, N], U32, name="w_codes", align_bytes=64)
         w_bytes = keep.tile([P, N], U8, name="w_bytes", align_bytes=64)
+        first_bytes = keep.tile([P, 128], U8, name="first_bytes", align_bytes=64)
+        nc.vector.tensor_copy(first_bytes[:], scale_table[:].indirect(entries(picked, 0, 128)))
         nc.vector.quantize_mx(out=w_codes[:].bitcast(FP8X4), scales=w_bytes[:], in_=w_grouped[:].rearrange("p n j -> p (n j)"))
-        picked_bytes = keep.tile([P, S], U8, name="picked_bytes", align_bytes=64)
+        later_bytes = keep.tile([P, S - 128], U8, name="later_bytes", tag="shared", align_bytes=64)
 
         lap_factor = keep.tile([P, 1], F32, name="lap_factor")
         log_factor = keep.tile([P, 1], F32, name="log_factor")
@@ -83,15 +85,18 @@ def tile_picked_ycahnh_log_p_kernel(tc, x_words, x_scales, w1, mob, offs, pos1, 
             nc.scalar.activation(shifted[:, lo:hi], banks[i][:], ACT.Sigmoid, bias=-math.log(19.0))
 
         for i, (lo, hi) in enumerate(PRODUCT_SLICES):
-            x_bytes = picked_bytes[:, lo:hi]
-            nc.vector.tensor_copy(x_bytes, scale_table[:].indirect(entries(picked, lo, hi)))
+            if i == 0:
+                x_bytes = first_bytes[:]
+            else:
+                x_bytes = later_bytes[:, lo - 128 : hi - 128]
+                nc.vector.tensor_copy(x_bytes, scale_table[:].indirect(entries(picked, lo, hi)))
             y = psum.tile([P, hi - lo], F32, name="y%d" % i)
             nc.tensor.matmul_mx(out=y[:], lhsT=w_codes[:].bitcast(FP8X4), lhsT_scale=w_bytes[:], rhs=x_codes[:, lo:hi].bitcast(FP8X4), rhs_scale=x_bytes, start=True, stop=True)
             nc.scalar.activation(sig[:, lo:hi], y[:], ACT.Sigmoid)
             banks.append(y)
-            if i < 1:
+            if i < 2:
                 shifted_sigmoid(i)
-        for i in (1, 2):
+        for i in (2, 3):
             shifted_sigmoid(i)
         for lo, hi in PRODUCT_SLICES:
             nc.vector.tensor_scalar(twice[:, lo:hi], sig[:, lo:hi], 2.0, None, ALU.mult)

from contextlib import ExitStack
import math

import concourse.mybir as mybir

K, T, S, N = 512, 1024, 512, 128
FLOPS = 2 * K * S * N

F32 = mybir.dt.float32
BF16 = mybir.dt.bfloat16
I32 = mybir.dt.int32
U32 = mybir.dt.uint32
U16 = mybir.dt.uint16
U8 = mybir.dt.uint8
FP8X4 = mybir.dt.float8_e4m3fn_x4
ACT = mybir.ActivationFunctionType
ALU = mybir.AluOpType

P = 128
PACK = 4
GROUP = 16
PRODUCT_SLICES = ((0, 128), (128, 256), (256, 384), (384, 512))
HALVES = ((0, 256), (256, 512))
STORE_SLICES = ((0, 256), (256, 416), (416, 512))


def tile_picked_ycahnh_log_p_kernel(tc, x_words, x_scales, w1, mob, offs, pos1, pos2, pos3, out):
    nc = tc.nc
    with ExitStack() as ctx:
        lists = ctx.enter_context(tc.tile_pool(name="lists", bufs=1))
        keep = ctx.enter_context(tc.tile_pool(name="keep", bufs=1))
        psum = ctx.enter_context(tc.psum_pool(name="psum", bufs=1))

        def entries(tile, lo, hi):
            return tile[:, lo // GROUP : hi // GROUP]

        word_table = keep.tile([P, T], I32, name="word_table", align_bytes=64)
        nc.sync.dma_start(out=word_table[:], in_=x_words[0].rearrange("p n t -> p (n t)").bitcast(I32))
        picked = lists.tile([P, S // GROUP], U16, name="picked")
        nc.sync.dma_start(picked[:], offs)
        scale_table = keep.tile([P, T], U8, name="scale_table", align_bytes=64)
        nc.vector.memset(scale_table[:].bitcast(I32), 0)
        scale_rows = x_scales[0].bitcast(I32)
        for q in range(4):
            nc.sync.dma_start(out=scale_table[32 * q : 32 * q + 4, :].bitcast(I32), in_=scale_rows[4 * q : 4 * q + 4, :])
        w_raw = keep.tile([P, PACK, N], F32, name="w_raw", tag="shared", align_bytes=64)
        nc.sync.dma_start(out=w_raw[:], in_=w1.rearrange("(p j) n -> p j n", j=PACK))
        neighbours = []
        for i, pos in enumerate((pos1, pos2, pos3)):
            tile = lists.tile([P, S // GROUP], U16, name="neighbours%d" % i)
            nc.sync.dma_start(tile[:], pos)
            neighbours.append(tile)
        mobility = keep.tile([P, 1], F32, name="mobility")
        nc.sync.dma_start(out=mobility[:], in_=mob)

        warm_in = keep.tile([P, 1], F32, name="warm_in")
        warm_out = keep.tile([P, 1], F32, name="warm_out")
        nc.gpsimd.memset(warm_in[:], 0.0)
        nc.scalar.activation(warm_out[:], warm_in[:], ACT.Sigmoid)

        x_codes = keep.tile([P, S], U32, name="x_codes", align_bytes=64)
        nc.vector.tensor_copy(x_codes[:], word_table[:].bitcast(U32).indirect(picked[:]))

        w_grouped = keep.tile([P, N, PACK], BF16, name="w_grouped", align_bytes=64)
        nc.scalar.copy(out=w_grouped[:], in_=w_raw[:].rearrange("p j n -> p n j"))
        w_codes = keep.tile([P, N], U32, name="w_codes", align_bytes=64)
        w_bytes = keep.tile([P, N], U8, name="w_bytes", align_bytes=64)
        first_bytes = keep.tile([P, 128], U8, name="first_bytes", align_bytes=64)
        nc.vector.tensor_copy(first_bytes[:], scale_table[:].indirect(entries(picked, 0, 128)))
        nc.vector.quantize_mx(out=w_codes[:].bitcast(FP8X4), scales=w_bytes[:], in_=w_grouped[:].rearrange("p n j -> p (n j)"))
        later_bytes = keep.tile([P, S - 128], U8, name="later_bytes", tag="shared", align_bytes=64)

        lap_factor = keep.tile([P, 1], F32, name="lap_factor")
        log_factor = keep.tile([P, 1], F32, name="log_factor")
        nc.gpsimd.tensor_scalar(lap_factor[:], mobility[:], -0.18, 0.0, ALU.mult, ALU.add)
        nc.gpsimd.tensor_scalar(log_factor[:], mobility[:], 0.4, 0.0, ALU.mult, ALU.add)

        sig = keep.tile([P, S], F32, name="sig")
        shifted = keep.tile([P, S], F32, name="shifted")
        twice = keep.tile([P, S], F32, name="twice")
        banks = []

        def shifted_sigmoid(i):
            lo, hi = PRODUCT_SLICES[i]
            nc.scalar.activation(shifted[:, lo:hi], banks[i][:], ACT.Sigmoid, bias=-math.log(19.0))

        for i, (lo, hi) in enumerate(PRODUCT_SLICES):
            if i == 0:
                x_bytes = first_bytes[:]
            else:
                x_bytes = later_bytes[:, lo - 128 : hi - 128]
                nc.vector.tensor_copy(x_bytes, scale_table[:].indirect(entries(picked, lo, hi)))
            y = psum.tile([P, hi - lo], F32, name="y%d" % i)
            nc.tensor.matmul_mx(out=y[:], lhsT=w_codes[:].bitcast(FP8X4), lhsT_scale=w_bytes[:], rhs=x_codes[:, lo:hi].bitcast(FP8X4), rhs_scale=x_bytes, start=True, stop=True)
            nc.scalar.activation(sig[:, lo:hi], y[:], ACT.Sigmoid)
            banks.append(y)
            if i < 2:
                shifted_sigmoid(i)
        for i in (2, 3):
            shifted_sigmoid(i)
        for lo, hi in PRODUCT_SLICES:
            nc.vector.tensor_scalar(twice[:, lo:hi], sig[:, lo:hi], 2.0, None, ALU.mult)

        log_ratio = keep.tile([P, S], F32, name="log_ratio")
        log_term = keep.tile([P, S], F32, name="log_term")
        con = keep.tile([P, S], F32, name="con")
        for lo, hi in HALVES:
            nc.scalar.activation(log_ratio[:, lo:hi], shifted[:, lo:hi], ACT.Ln, bias=1.0 / 19.0, scale=360.0 / 19.0)
            nc.scalar.activation(log_term[:, lo:hi], log_ratio[:, lo:hi], ACT.Copy, scale=log_factor[:])
        for lo, hi in HALVES:
            nc.scalar.activation(con[:, lo:hi], sig[:, lo:hi], ACT.Copy, scale=0.9)

        def add_neighbours(window, start, name, last_slices):
            total = start
            for i, places in enumerate(neighbours):
                following = keep.tile([P, S], F32, name="%s%d" % (name, i))
                for lo, hi in last_slices if i == 2 else HALVES:
                    nc.vector.tensor_tensor(following[:, lo:hi], window[:].indirect(entries(places, lo, hi)), total[:, lo:hi], ALU.add)
                total = following
            return total

        sig_sum = add_neighbours(sig, twice, "sig_sum", HALVES)
        flux = keep.tile([P, S], F32, name="flux")
        base = keep.tile([P, S], F32, name="base")
        for lo, hi in HALVES:
            nc.vector.scalar_tensor_tensor(flux[:, lo:hi], sig_sum[:, lo:hi], lap_factor[:], log_term[:, lo:hi], ALU.mult, ALU.add)
        for lo, hi in HALVES:
            nc.vector.scalar_tensor_tensor(base[:, lo:hi], flux[:, lo:hi], -3.0, con[:, lo:hi], ALU.mult, ALU.add)
        result = add_neighbours(flux, base, "result", STORE_SLICES)
        for lo, hi in STORE_SLICES:
            nc.sync.dma_start(out=out[:, lo:hi], in_=result[:, lo:hi])
